import numpy as np
import ml_dtypes


def mxq(x, axis, fmt="e4m3"):
    dtype, down = {"e4m3": (ml_dtypes.float8_e4m3fn, 7), "e5m2": (ml_dtypes.float8_e5m2, 14)}[fmt]
    v = np.moveaxis(np.asarray(x, np.float32).astype(ml_dtypes.bfloat16).astype(np.float64), axis, -1)
    blocks = v.reshape(v.shape[:-1] + (-1, 32))
    amax = np.abs(blocks).max(-1, keepdims=True)
    byte = np.maximum(np.where(amax > 0, np.frexp(amax)[1] - 1 + 127, 0) - down, 1)
    scale = np.exp2(byte - 127.0)
    codes = (blocks / scale).astype(np.float32).astype(dtype).astype(np.float64)
    return np.moveaxis((codes * scale).reshape(v.shape), -1, axis)


WIDE = False


def mx_kscale(k):
    if not WIDE:
        return np.ones(k)
    levels = np.array([10, -10, 5, -5, 0])
    if k % 512:
        return np.exp2(np.random.permutation(np.resize(levels, k // 32))).repeat(32)
    a = np.empty((k // 512, 16))
    for p in range(k // 512):
        a[p, :8] = np.random.permutation(np.resize(levels, 8))
        for g in range(8):
            far = levels[np.abs(levels - a[p, g]) >= 10]
            a[p, g + 8] = far[np.random.randint(len(far))]
    return np.exp2(a.ravel()).repeat(32)


def f64(x):
    return np.asarray(x).astype(np.float64)


def striped(idx):
    return np.tile(idx.reshape(-1, 16).T, (8, 1)).astype(np.uint16)


def unstriped(offs):
    return offs[:16].T.reshape(-1).astype(np.int64)


def pack_weight(w):
    k, n = w.shape
    w = f64(np.asarray(w, np.float32).astype(ml_dtypes.bfloat16)).reshape(k // 32, 32, n)
    amax = np.abs(w).max(1)
    byte = np.clip(np.where(amax > 0, np.frexp(amax)[1] - 1 + 127 - 7, 1), 1, 254)
    scaled = (w * np.exp2(127.0 - byte)[:, None, :]).reshape(k, n).astype(np.float32)
    words = np.ascontiguousarray(scaled.reshape(k // 512, 128, 4, n).transpose(0, 1, 3, 2)).astype(ml_dtypes.float8_e4m3fn).view(np.uint8)
    return words, np.ascontiguousarray(byte.astype(np.uint8).reshape(k // 512, 16, n))


def unpack_weight(words, scales):
    g, p, n, _ = words.shape
    vals = np.ascontiguousarray(words).view(ml_dtypes.float8_e4m3fn).astype(np.float64) * np.repeat(np.exp2(scales.astype(np.float64) - 127.0), 8, axis=1)[..., None]
    return vals.transpose(0, 1, 3, 2).reshape(g * 512, n)


def sigmoid(v):
    return 1.0 / (1.0 + np.exp(-np.maximum(v, -700.0)))


K, T, S, N, V = 1024, 1024, 512, 128, 256
P = 2 ** 7


def setup_inputs():
    n = np.random.standard_normal
    s = mx_kscale(K)[:, None]
    packed_xT = pack_weight(n((K, T)) * s)
    return {
        "x_words": packed_xT[0],
        "x_scales": packed_xT[1],
        "w1": (n((K, N)) / np.sqrt(K) / s).astype(np.float32),
        "w2": (n((K, N)) / np.sqrt(K) / s).astype(np.float32),
        "w3": (n((K, N)) / np.sqrt(K) / s).astype(np.float32),
        "air": (np.random.uniform(0.8, 1.0, (N, 1))).astype(np.float32),
        "tmin": (np.tile(np.random.uniform(0.35, 0.65, V), (P, 1))).astype(np.float32),
        "beta": (np.tile(-np.random.uniform(0.5, 2.0, V), (P, 1))).astype(np.float32),
        "offs": striped(np.random.permutation(T)[:S]),
        "pos1": striped(np.random.permutation(S)[:V]),
        "pos2": striped(np.random.permutation(S)[:V]),
        "cen": striped(np.random.permutation(S)[:V]),
    }


def reference(x_words, x_scales, w1, w2, w3, air, tmin, beta, offs, pos1, pos2, cen):
    xq = unpack_weight(x_words, x_scales)[:, unstriped(offs)]
    yr = mxq(f64(w1), 0, "e4m3").T @ xq
    red = sigmoid(yr + 1.5)
    yg = mxq(f64(w2), 0, "e4m3").T @ xq
    grn = sigmoid(yg + 1.5)
    yb = mxq(f64(w3), 0, "e4m3").T @ xq
    blu = sigmoid(yb + 1.5)
    dark = np.minimum(np.minimum(red, grn), blu)
    mn = np.minimum(np.minimum(dark[:, unstriped(cen)], dark[:, unstriped(pos1)]), dark[:, unstriped(pos2)])
    tr = np.maximum(-1.0 * (0.95 * (mn / (0.2 * mn + f64(air)))) + 1.0, f64(tmin)[:1])
    return np.log(tr) * f64(beta)[:1] + 0.4 * (grn[:, unstriped(cen)] - blu[:, unstriped(cen)])

@@ -1,0 +1,199 @@
+from contextlib import ExitStack
+
+import concourse.mybir as mybir
+
+K, T, S, N, V = 1024, 1024, 512, 128, 256
+FLOPS = 3 * 2 * K * N * S
+
+F32 = mybir.dt.float32
+BF16 = mybir.dt.bfloat16
+I32 = mybir.dt.int32
+U32 = mybir.dt.uint32
+U16 = mybir.dt.uint16
+U8 = mybir.dt.uint8
+FP8X4 = mybir.dt.float8_e4m3fn_x4
+ALU = mybir.AluOpType
+ACT = mybir.ActivationFunctionType
+
+P = 128
+PACK = 4
+PASSES = K // (P * PACK)
+LANES = 16
+HALF_S = S // 2
+HALF_V = V // 2
+
+
+def tile_picked_ydehz_depth_p_kernel(
+    tc, x_words, x_scales, w1, w2, w3, air, tmin, beta, offs, pos1, pos2, cen, out
+):
+    nc = tc.nc
+    with ExitStack() as ctx:
+        sb = ctx.enter_context(tc.tile_pool(name="sb", bufs=1))
+        ps = ctx.enter_context(tc.psum_pool(name="ps", bufs=1))
+
+        def sbuf(name, shape, dtype):
+            return sb.tile(shape, dtype, name=name, align_bytes=64)
+
+        def load_list(name, src):
+            t = sbuf(name, list(src.shape), U16)
+            nc.sync.dma_start(t[:], src)
+            return t
+
+        def load_words(o):
+            t = sbuf("x_words%d" % o, [P, T], I32)
+            nc.sync.dma_start(t[:], x_words[o].rearrange("p n t -> p (n t)").bitcast(I32))
+            return t
+
+        def load_weight(name, w, o):
+            t = sbuf("%s_raw%d" % (name, o), [P, PACK, N], F32)
+            rows = w[o * P * PACK : (o + 1) * P * PACK, :]
+            nc.sync.dma_start(t[:], rows.rearrange("(p j) m -> p j m", j=PACK))
+            return t
+
+        def round_weight(name, raw, on_scalar):
+            t = sbuf(name + "_bf16", [P, N, PACK], BF16)
+            dst = t[:].rearrange("p (c i) j -> p c j i", i=4)
+            src = raw[:].rearrange("p j (c i) -> p c j i", i=4)
+            if on_scalar:
+                nc.scalar.activation(dst, src, ACT.Copy)
+            else:
+                nc.vector.tensor_copy(dst, src)
+            return t
+
+        def quantise(name, rounded):
+            codes = sbuf(name + "_codes", [P, N], U32)
+            scales = sbuf(name + "_scales", [P, N], U8)
+            nc.vector.quantize_mx(
+                out=codes[:].bitcast(FP8X4), scales=scales[:], in_=rounded[:].rearrange("p m j -> p (m j)")
+            )
+            return codes, scales
+
+        scale_table = sbuf("scale_table", [P, T], U8)
+        nc.vector.memset(scale_table[:].bitcast(I32), 0)
+        offs_t = load_list("offs_t", offs)
+        words0 = load_words(0)
+        for q in range(4):
+            nc.scalar.dma_start(
+                scale_table[32 * q : 32 * q + 4 * PASSES, :].bitcast(I32),
+                x_scales[:, 4 * q : 4 * q + 4, :].bitcast(I32),
+            )
+        raw_b = [load_weight("w3", w3, o) for o in range(PASSES)]
+        words1 = load_words(1)
+        raw_g = [load_weight("w2", w2, o) for o in range(PASSES)]
+        raw_r = [load_weight("w1", w1, o) for o in range(PASSES)]
+        air_t = sbuf("air_t", [P, 1], F32)
+        nc.gpsimd.dma_start(air_t[:], air)
+        cen_t = load_list("cen_t", cen)
+        pos1_t = load_list("pos1_t", pos1)
+        pos2_t = load_list("pos2_t", pos2)
+        tmin_t = sbuf("tmin_t", [P, V], F32)
+        nc.sync.dma_start(tmin_t[:], tmin)
+        beta_t = sbuf("beta_t", [P, V], F32)
+        nc.sync.dma_start(beta_t[:], beta)
+
+        shift = sbuf("shift", [P, 1], F32)
+        nc.gpsimd.tensor_scalar(shift[:], air_t[:], 10.0, 1.0, ALU.mult, ALU.add)
+        root = sbuf("root", [P, 1], F32)
+        nc.gpsimd.tensor_scalar(root[:], air_t[:], 38.0 / 3.0, 0.0, ALU.mult, ALU.add)
+
+        def gather_words(o, words):
+            t = sbuf("picked_words%d" % o, [P, S], U32)
+            nc.vector.tensor_copy(t[:], words[:].bitcast(U32).indirect(offs_t[:]))
+            return t
+
+        picked0 = gather_words(0, words0)
+        picked_scales = sbuf("picked_scales", [P, S], U8)
+        nc.vector.tensor_copy(picked_scales[:], scale_table[:].indirect(offs_t[:]))
+
+        def product(bank, q, picked, o, cols):
+            codes, scales = q
+            nc.tensor.matmul_mx(
+                out=bank[:],
+                lhsT=codes[:].bitcast(FP8X4),
+                lhsT_scale=scales[:],
+                rhs=picked[:, cols].bitcast(FP8X4),
+                rhs_scale=picked_scales[4 * o : P, cols],
+                start=(o == 0),
+                stop=(o == PASSES - 1),
+            )
+
+        every = slice(0, S)
+        bank_b = ps.tile([P, S], F32, name="bank_b")
+        bank_g = ps.tile([P, S], F32, name="bank_g")
+        bank_r = [ps.tile([P, HALF_S], F32, name="bank_r%d" % h) for h in range(2)]
+        halves = [slice(h * HALF_S, (h + 1) * HALF_S) for h in range(2)]
+
+        q_b = [quantise("w3_%d" % o, round_weight("w3_%d" % o, raw_b[o], True)) for o in range(PASSES)]
+        product(bank_b, q_b[0], picked0, 0, every)
+        picked1 = gather_words(1, words1)
+        product(bank_b, q_b[1], picked1, 1, every)
+        picked = [picked0, picked1]
+        for o in range(PASSES):
+            q = quantise("w2_%d" % o, round_weight("w2_%d" % o, raw_g[o], True))
+            product(bank_g, q, picked[o], o, every)
+        blu = sbuf("blu", [P, S], F32)
+        nc.scalar.activation(blu[:], bank_b[:], ACT.Tanh, bias=0.75, scale=0.5)
+        for o in range(PASSES):
+            q = quantise("w1_%d" % o, round_weight("w1_%d" % o, raw_r[o], False))
+            for h in range(2):
+                product(bank_r[h], q, picked[o], o, halves[h])
+        grn = sbuf("grn", [P, S], F32)
+        nc.scalar.activation(grn[:], bank_g[:], ACT.Tanh, bias=0.75, scale=0.5)
+        blu_shifted = sbuf("blu_shifted", [P, S], F32)
+        nc.vector.tensor_scalar(blu_shifted[:], blu[:], shift[:], None, ALU.add)
+        blu_cen = sbuf("blu_cen", [P, V], F32)
+        nc.scalar.activation(blu_cen[:], blu[:].indirect(cen_t[:]), ACT.Copy)
+        low = sbuf("low", [P, S], F32)
+        nc.vector.scalar_tensor_tensor(low[:], grn[:], shift[:], blu_shifted[:], ALU.add, ALU.min)
+        red = [sbuf("red%d" % h, [P, HALF_S], F32) for h in range(2)]
+        dark = sbuf("dark", [P, S], F32)
+        for h in range(2):
+            nc.scalar.activation(red[h][:], bank_r[h][:], ACT.Tanh, bias=0.75, scale=0.5)
+        colour = sbuf("colour", [P, V], F32)
+        nc.vector.tensor_tensor(colour[:], grn[:].indirect(cen_t[:]), blu_cen[:], ALU.subtract)
+        for h in range(2):
+            nc.vector.scalar_tensor_tensor(
+                dark[:, halves[h]], red[h][:], shift[:], low[:, halves[h]], ALU.add, ALU.min
+            )
+
+        def part(name):
+            return [sbuf("%s%d" % (name, h), [P, HALF_V], F32) for h in range(2)]
+
+        def fetch(dst, lst, h, on_scalar):
+            w = HALF_V // LANES
+            src = dark[:].indirect(lst[:, h * w : (h + 1) * w])
+            if on_scalar:
+                nc.scalar.activation(dst[:], src, ACT.Copy)
+            else:
+                nc.vector.tensor_copy(dst[:], src)
+
+        g0, g1, g2, x, d, pn, r, lg, lb, res = [part(n) for n in ("g0", "g1", "g2", "x", "d", "pn", "r", "lg", "lb", "res")]
+        pair = [sbuf("pair%d" % h, [P, 2, HALF_V], F32) for h in range(2)]
+        logs = [sbuf("logs%d" % h, [P, 2, HALF_V], F32) for h in range(2)]
+        cols = [slice(h * HALF_V, (h + 1) * HALF_V) for h in range(2)]
+        fetch(g0[0], cen_t, 0, True)
+        fetch(g2[0], pos2_t, 0, False)
+        fetch(g1[0], pos1_t, 0, True)
+        fetch(g2[1], pos2_t, 1, False)
+        fetch(g0[1], cen_t, 1, True)
+        fetch(g1[1], pos1_t, 1, False)
+        for h in range(2):
+            nc.vector.tensor_tensor(x[h][:], g2[h][:], g1[h][:], ALU.min)
+        for h in range(2):
+            nc.vector.tensor_tensor(d[h][:], x[h][:], g0[h][:], ALU.min)
+        for h in range(2):
+            nc.vector.tensor_tensor(pair[h][:, 0, :], d[h][:], d[h][:], ALU.mult)
+        for h in range(2):
+            nc.vector.scalar_tensor_tensor(pn[h][:], d[h][:], root[:], d[h][:], ALU.subtract, ALU.mult)
+        for h in range(2):
+            nc.vector.tensor_tensor(r[h][:], pair[h][:, 0, :], tmin_t[:, cols[h]], ALU.mult)
+        for h in range(2):
+            nc.vector.scalar_tensor_tensor(pair[h][:, 1, :], pn[h][:], -3.75, r[h][:], ALU.mult, ALU.max)
+            nc.scalar.activation(logs[h][:], pair[h][:], ACT.Ln)
+        for h in range(2):
+            nc.vector.tensor_tensor(lg[h][:], logs[h][:, 1, :], logs[h][:, 0, :], ALU.subtract)
+        for h in range(2):
+            nc.vector.tensor_tensor(lb[h][:], lg[h][:], beta_t[:, cols[h]], ALU.mult)
+        for h in range(2):
+            nc.vector.scalar_tensor_tensor(res[h][:], colour[:, cols[h]], 0.2, lb[h][:], ALU.mult, ALU.add)
+            nc.sync.dma_start(out[:, cols[h]], res[h][:])

@@ -32,7 +32,7 @@ def tile_picked_ydehz_depth_p_kernel(
         ps = ctx.enter_context(tc.psum_pool(name="ps", bufs=1))
 
         def sbuf(name, shape, dtype):
-            return sb.tile(shape, dtype, name=name, align_bytes=64)
+            return sb.tile(shape, dtype, name=name, tag=name, align_bytes=64)
 
         def load_list(name, src):
             t = sbuf(name, list(src.shape), U16)
@@ -60,8 +60,8 @@ def tile_picked_ydehz_depth_p_kernel(
                 nc.vector.tensor_copy(dst, src)
             return t
 
-        def quantise(name, rounded):
-            codes = sbuf(name + "_codes", [P, N], U32)
+        def quantise(name, rounded, tag=None):
+            codes = sb.tile([P, N], U32, name=name + "_codes", tag=tag or name + "_codes", align_bytes=64)
             scales = sbuf(name + "_scales", [P, N], U8)
             nc.vector.quantize_mx(
                 out=codes[:].bitcast(FP8X4), scales=scales[:], in_=rounded[:].rearrange("p m j -> p (m j)")
@@ -71,18 +71,21 @@ def tile_picked_ydehz_depth_p_kernel(
         scale_table = sbuf("scale_table", [P, T], U8)
         nc.vector.memset(scale_table[:].bitcast(I32), 0)
         offs_t = load_list("offs_t", offs)
-        words0 = load_words(0)
+        raw_b0 = load_weight("w3", w3, 0)
         for q in range(4):
-            nc.scalar.dma_start(
+            nc.sync.dma_start(
                 scale_table[32 * q : 32 * q + 4 * PASSES, :].bitcast(I32),
                 x_scales[:, 4 * q : 4 * q + 4, :].bitcast(I32),
             )
-        raw_b = [load_weight("w3", w3, o) for o in range(PASSES)]
-        words1 = load_words(1)
-        raw_g = [load_weight("w2", w2, o) for o in range(PASSES)]
-        raw_r = [load_weight("w1", w1, o) for o in range(PASSES)]
+        words0 = load_words(0)
         air_t = sbuf("air_t", [P, 1], F32)
-        nc.gpsimd.dma_start(air_t[:], air)
+        nc.sync.dma_start(air_t[:], air)
+        raw_g0 = load_weight("w2", w2, 0)
+        words1 = load_words(1)
+        raw_b1 = load_weight("w3", w3, 1)
+        raw_g1 = load_weight("w2", w2, 1)
+        raw_r0 = load_weight("w1", w1, 0)
+        raw_r1 = load_weight("w1", w1, 1)
         cen_t = load_list("cen_t", cen)
         pos1_t = load_list("pos1_t", pos1)
         pos2_t = load_list("pos2_t", pos2)
@@ -101,7 +104,6 @@ def tile_picked_ydehz_depth_p_kernel(
             nc.vector.tensor_copy(t[:], words[:].bitcast(U32).indirect(offs_t[:]))
             return t
 
-        picked0 = gather_words(0, words0)
         picked_scales = sbuf("picked_scales", [P, S], U8)
         nc.vector.tensor_copy(picked_scales[:], scale_table[:].indirect(offs_t[:]))
 
@@ -117,83 +119,108 @@ def tile_picked_ydehz_depth_p_kernel(
                 stop=(o == PASSES - 1),
             )
 
+        RP = 2
+        RW = S // RP
         every = slice(0, S)
         bank_b = ps.tile([P, S], F32, name="bank_b")
         bank_g = ps.tile([P, S], F32, name="bank_g")
-        bank_r = [ps.tile([P, HALF_S], F32, name="bank_r%d" % h) for h in range(2)]
-        halves = [slice(h * HALF_S, (h + 1) * HALF_S) for h in range(2)]
+        bank_r = [ps.tile([P, RW], F32, name="bank_r%d" % h) for h in range(RP)]
+        halves = [slice(h * RW, (h + 1) * RW) for h in range(RP)]
 
-        q_b = [quantise("w3_%d" % o, round_weight("w3_%d" % o, raw_b[o], True)) for o in range(PASSES)]
-        product(bank_b, q_b[0], picked0, 0, every)
+        q = quantise("w3_0", round_weight("w3_0", raw_b0, True))
+        picked0 = gather_words(0, words0)
+        product(bank_b, q, picked0, 0, every)
+        q = quantise("w2_0", round_weight("w2_0", raw_g0, True))
+        product(bank_g, q, picked0, 0, every)
         picked1 = gather_words(1, words1)
-        product(bank_b, q_b[1], picked1, 1, every)
-        picked = [picked0, picked1]
-        for o in range(PASSES):
-            q = quantise("w2_%d" % o, round_weight("w2_%d" % o, raw_g[o], True))
-            product(bank_g, q, picked[o], o, every)
-        blu = sbuf("blu", [P, S], F32)
+        q = quantise("w3_1", round_weight("w3_1", raw_b1, True))
+        product(bank_b, q, picked1, 1, every)
+        q = quantise("w2_1", round_weight("w2_1", raw_g1, True))
+        product(bank_g, q, picked1, 1, every)
+        rounded_r0 = round_weight("w1_0", raw_r0, True)
+        rounded_r1 = round_weight("w1_1", raw_r1, False)
+        q0 = quantise("w1_0", rounded_r0)
+        q1 = quantise("w1_1", rounded_r1, "last")
+        for h in range(RP):
+            product(bank_r[h], q0, picked0, 0, halves[h])
+        for h in range(RP):
+            product(bank_r[h], q1, picked1, 1, halves[h])
+        blu = sb.tile([P, S], F32, name="blu", tag="w1_raw0", align_bytes=64)
         nc.scalar.activation(blu[:], bank_b[:], ACT.Tanh, bias=0.75, scale=0.5)
-        for o in range(PASSES):
-            q = quantise("w1_%d" % o, round_weight("w1_%d" % o, raw_r[o], False))
-            for h in range(2):
-                product(bank_r[h], q, picked[o], o, halves[h])
         grn = sbuf("grn", [P, S], F32)
-        nc.scalar.activation(grn[:], bank_g[:], ACT.Tanh, bias=0.75, scale=0.5)
-        blu_shifted = sbuf("blu_shifted", [P, S], F32)
-        nc.vector.tensor_scalar(blu_shifted[:], blu[:], shift[:], None, ALU.add)
-        blu_cen = sbuf("blu_cen", [P, V], F32)
-        nc.scalar.activation(blu_cen[:], blu[:].indirect(cen_t[:]), ACT.Copy)
-        low = sbuf("low", [P, S], F32)
-        nc.vector.scalar_tensor_tensor(low[:], grn[:], shift[:], blu_shifted[:], ALU.add, ALU.min)
-        red = [sbuf("red%d" % h, [P, HALF_S], F32) for h in range(2)]
-        dark = sbuf("dark", [P, S], F32)
-        for h in range(2):
+        for h in range(RP):
+            nc.scalar.activation(grn[:, halves[h]], bank_g[:, halves[h]], ACT.Tanh, bias=0.75, scale=0.5)
+        red = [sbuf("red%d" % h, [P, RW], F32) for h in range(RP)]
+        for h in range(RP):
             nc.scalar.activation(red[h][:], bank_r[h][:], ACT.Tanh, bias=0.75, scale=0.5)
-        colour = sbuf("colour", [P, V], F32)
-        nc.vector.tensor_tensor(colour[:], grn[:].indirect(cen_t[:]), blu_cen[:], ALU.subtract)
-        for h in range(2):
+        blu_cen = sb.tile([P, V], F32, name="blu_cen", tag="last", align_bytes=64)
+        nc.scalar.activation(blu_cen[:], blu[:].indirect(cen_t[:]), ACT.Copy)
+        blu_shifted = sb.tile([P, S], F32, name="blu_shifted", tag="w1_1_bf16", align_bytes=64)
+        nc.vector.tensor_scalar(blu_shifted[:], blu[:], shift[:], None, ALU.add)
+        low = [sbuf("low%d" % h, [P, RW], F32) for h in range(RP)]
+        for h in range(RP):
             nc.vector.scalar_tensor_tensor(
-                dark[:, halves[h]], red[h][:], shift[:], low[:, halves[h]], ALU.add, ALU.min
+                low[h][:], grn[:, halves[h]], shift[:], blu_shifted[:, halves[h]], ALU.add, ALU.min
             )
+        dark = sbuf("dark", [P, S], F32)
+        for h in range(RP):
+            nc.vector.scalar_tensor_tensor(dark[:, halves[h]], red[h][:], shift[:], low[h][:], ALU.add, ALU.min)
+
+        NP = 4
+        W = V // NP
 
         def part(name):
-            return [sbuf("%s%d" % (name, h), [P, HALF_V], F32) for h in range(2)]
+            return [sbuf("%s%d" % (name, h), [P, W], F32) for h in range(NP)]
 
-        def fetch(dst, lst, h, on_scalar):
+        def fetch(name, lst, h, on_scalar):
+            dst = sbuf("%s%d" % (name, h), [P, HALF_V], F32)
             w = HALF_V // LANES
             src = dark[:].indirect(lst[:, h * w : (h + 1) * w])
             if on_scalar:
                 nc.scalar.activation(dst[:], src, ACT.Copy)
             else:
                 nc.vector.tensor_copy(dst[:], src)
+            return dst
 
-        g0, g1, g2, x, d, pn, r, lg, lb, res = [part(n) for n in ("g0", "g1", "g2", "x", "d", "pn", "r", "lg", "lb", "res")]
-        pair = [sbuf("pair%d" % h, [P, 2, HALF_V], F32) for h in range(2)]
-        logs = [sbuf("logs%d" % h, [P, 2, HALF_V], F32) for h in range(2)]
-        cols = [slice(h * HALF_V, (h + 1) * HALF_V) for h in range(2)]
-        fetch(g0[0], cen_t, 0, True)
-        fetch(g2[0], pos2_t, 0, False)
-        fetch(g1[0], pos1_t, 0, True)
-        fetch(g2[1], pos2_t, 1, False)
-        fetch(g0[1], cen_t, 1, True)
-        fetch(g1[1], pos1_t, 1, False)
-        for h in range(2):
-            nc.vector.tensor_tensor(x[h][:], g2[h][:], g1[h][:], ALU.min)
-        for h in range(2):
-            nc.vector.tensor_tensor(d[h][:], x[h][:], g0[h][:], ALU.min)
-        for h in range(2):
+        x, d, pn, lg, lb = [part(n) for n in ("x", "d", "pn", "lg", "lb")]
+        res = [sbuf("res%d" % h, [P, HALF_V], F32) for h in range(2)]
+        r = [sb.tile([P, V], F32, name="r0", tag="floor_then_colour")] + part("r")[1:]
+        pair = [sbuf("pair%d" % h, [P, 2, W], F32) for h in range(NP)]
+        logs = [sbuf("logs%d" % h, [P, 2, W], F32) for h in range(NP)]
+        cols = [slice(h * W, (h + 1) * W) for h in range(NP)]
+        g0, g1, g2 = [], [], []
+        g0.append(fetch("g0", cen_t, 0, True))
+        g2.append(fetch("g2", pos2_t, 0, False))
+        g1.append(fetch("g1", pos1_t, 0, True))
+        g2.append(fetch("g2", pos2_t, 1, False))
+        g0.append(fetch("g0", cen_t, 1, True))
+        g1.append(fetch("g1", pos1_t, 1, False))
+
+        def piece(g, h):
+            per = NP // 2
+            return g[h // per][:, (h % per) * W : (h % per + 1) * W]
+
+        for h in range(NP):
+            nc.vector.tensor_tensor(x[h][:], piece(g2, h), piece(g0 if h < NP // 2 else g1, h), ALU.min)
+        for h in range(NP):
+            nc.vector.tensor_tensor(d[h][:], x[h][:], piece(g1 if h < NP // 2 else g0, h), ALU.min)
+        for h in range(NP):
             nc.vector.tensor_tensor(pair[h][:, 0, :], d[h][:], d[h][:], ALU.mult)
-        for h in range(2):
+        for h in range(NP):
             nc.vector.scalar_tensor_tensor(pn[h][:], d[h][:], root[:], d[h][:], ALU.subtract, ALU.mult)
-        for h in range(2):
-            nc.vector.tensor_tensor(r[h][:], pair[h][:, 0, :], tmin_t[:, cols[h]], ALU.mult)
-        for h in range(2):
-            nc.vector.scalar_tensor_tensor(pair[h][:, 1, :], pn[h][:], -3.75, r[h][:], ALU.mult, ALU.max)
+        for h in range(NP):
+            nc.vector.tensor_tensor(r[h][:, 0:W], pair[h][:, 0, :], tmin_t[:, cols[h]], ALU.mult)
+        for h in range(NP):
+            nc.vector.scalar_tensor_tensor(pair[h][:, 1, :], pn[h][:], -3.75, r[h][:, 0:W], ALU.mult, ALU.max)
             nc.scalar.activation(logs[h][:], pair[h][:], ACT.Ln)
-        for h in range(2):
+        colour = sb.tile([P, V], F32, name="colour", tag="floor_then_colour")
+        nc.vector.tensor_tensor(colour[:], grn[:].indirect(cen_t[:]), blu_cen[:], ALU.subtract)
+        for h in range(NP):
             nc.vector.tensor_tensor(lg[h][:], logs[h][:, 1, :], logs[h][:, 0, :], ALU.subtract)
-        for h in range(2):
+        for h in range(NP):
             nc.vector.tensor_tensor(lb[h][:], lg[h][:], beta_t[:, cols[h]], ALU.mult)
-        for h in range(2):
-            nc.vector.scalar_tensor_tensor(res[h][:], colour[:, cols[h]], 0.2, lb[h][:], ALU.mult, ALU.add)
-            nc.sync.dma_start(out[:, cols[h]], res[h][:])
+        for h in range(NP):
+            nc.vector.scalar_tensor_tensor(piece(res, h), colour[:, cols[h]], 0.2, lb[h][:], ALU.mult, ALU.add)
+            if (h + 1) % (NP // 2) == 0:
+                u = h // (NP // 2)
+                nc.sync.dma_start(out[:, u * HALF_V : (u + 1) * HALF_V], res[u][:])

@@ -81,8 +81,8 @@ def tile_picked_ydehz_depth_p_kernel(
         air_t = sbuf("air_t", [P, 1], F32)
         nc.sync.dma_start(air_t[:], air)
         raw_g0 = load_weight("w2", w2, 0)
-        words1 = load_words(1)
         raw_b1 = load_weight("w3", w3, 1)
+        words1 = load_words(1)
         raw_g1 = load_weight("w2", w2, 1)
         raw_r0 = load_weight("w1", w1, 0)
         raw_r1 = load_weight("w1", w1, 1)
@@ -119,52 +119,55 @@ def tile_picked_ydehz_depth_p_kernel(
                 stop=(o == PASSES - 1),
             )
 
-        RP = 2
-        RW = S // RP
         every = slice(0, S)
-        bank_b = ps.tile([P, S], F32, name="bank_b")
+        bank_b = [ps.tile([P, HALF_S], F32, name="bank_b%d" % h) for h in range(2)]
         bank_g = ps.tile([P, S], F32, name="bank_g")
-        bank_r = [ps.tile([P, RW], F32, name="bank_r%d" % h) for h in range(RP)]
-        halves = [slice(h * RW, (h + 1) * RW) for h in range(RP)]
+        halves = [slice(0, HALF_S), slice(HALF_S, S)]
+        pieces = [slice(0, 256), slice(256, 512)]
+        bank_r = [ps.tile([P, c.stop - c.start], F32, name="bank_r%d" % c.start) for c in pieces]
 
         q = quantise("w3_0", round_weight("w3_0", raw_b0, True))
         picked0 = gather_words(0, words0)
-        product(bank_b, q, picked0, 0, every)
+        for bank, c in zip(bank_b, halves):
+            product(bank, q, picked0, 0, c)
         q = quantise("w2_0", round_weight("w2_0", raw_g0, True))
         product(bank_g, q, picked0, 0, every)
-        picked1 = gather_words(1, words1)
         q = quantise("w3_1", round_weight("w3_1", raw_b1, True))
-        product(bank_b, q, picked1, 1, every)
+        picked1 = sbuf("picked_words1", [P, S], U32)
+        for bank, c in zip(bank_b, halves):
+            entries = offs_t[:, c.start // LANES : c.stop // LANES]
+            nc.vector.tensor_copy(picked1[:, c], words1[:].bitcast(U32).indirect(entries))
+            product(bank, q, picked1, 1, c)
         q = quantise("w2_1", round_weight("w2_1", raw_g1, True))
         product(bank_g, q, picked1, 1, every)
         rounded_r0 = round_weight("w1_0", raw_r0, True)
         rounded_r1 = round_weight("w1_1", raw_r1, False)
         q0 = quantise("w1_0", rounded_r0)
         q1 = quantise("w1_1", rounded_r1, "last")
-        for h in range(RP):
-            product(bank_r[h], q0, picked0, 0, halves[h])
-        for h in range(RP):
-            product(bank_r[h], q1, picked1, 1, halves[h])
+        for bank, c in zip(bank_r, pieces):
+            product(bank, q0, picked0, 0, c)
+        for bank, c in zip(bank_r, pieces):
+            product(bank, q1, picked1, 1, c)
         blu = sb.tile([P, S], F32, name="blu", tag="w1_raw0", align_bytes=64)
-        nc.scalar.activation(blu[:], bank_b[:], ACT.Tanh, bias=0.75, scale=0.5)
+        for bank, c in zip(bank_b, halves):
+            nc.scalar.activation(blu[:, c], bank[:], ACT.Tanh, bias=0.75, scale=0.5)
         grn = sbuf("grn", [P, S], F32)
-        for h in range(RP):
-            nc.scalar.activation(grn[:, halves[h]], bank_g[:, halves[h]], ACT.Tanh, bias=0.75, scale=0.5)
-        red = [sbuf("red%d" % h, [P, RW], F32) for h in range(RP)]
-        for h in range(RP):
-            nc.scalar.activation(red[h][:], bank_r[h][:], ACT.Tanh, bias=0.75, scale=0.5)
+        for c in halves:
+            nc.scalar.activation(grn[:, c], bank_g[:, c], ACT.Tanh, bias=0.75, scale=0.5)
+        red = sbuf("red", [P, S], F32)
+        for bank, c in zip(bank_r, pieces):
+            nc.scalar.activation(red[:, c], bank[:], ACT.Tanh, bias=0.75, scale=0.5)
         blu_cen = sb.tile([P, V], F32, name="blu_cen", tag="last", align_bytes=64)
         nc.scalar.activation(blu_cen[:], blu[:].indirect(cen_t[:]), ACT.Copy)
         blu_shifted = sb.tile([P, S], F32, name="blu_shifted", tag="w1_1_bf16", align_bytes=64)
-        nc.vector.tensor_scalar(blu_shifted[:], blu[:], shift[:], None, ALU.add)
-        low = [sbuf("low%d" % h, [P, RW], F32) for h in range(RP)]
-        for h in range(RP):
-            nc.vector.scalar_tensor_tensor(
-                low[h][:], grn[:, halves[h]], shift[:], blu_shifted[:, halves[h]], ALU.add, ALU.min
-            )
+        for c in halves:
+            nc.vector.tensor_scalar(blu_shifted[:, c], blu[:, c], shift[:], None, ALU.add)
+        low = sbuf("low", [P, S], F32)
+        for c in halves:
+            nc.vector.scalar_tensor_tensor(low[:, c], grn[:, c], shift[:], blu_shifted[:, c], ALU.add, ALU.min)
         dark = sbuf("dark", [P, S], F32)
-        for h in range(RP):
-            nc.vector.scalar_tensor_tensor(dark[:, halves[h]], red[h][:], shift[:], low[h][:], ALU.add, ALU.min)
+        for c in pieces:
+            nc.vector.scalar_tensor_tensor(dark[:, c], red[:, c], shift[:], low[:, c], ALU.add, ALU.min)
 
         NP = 4
         W = V // NP

from contextlib import ExitStack

import concourse.mybir as mybir

K, T, S, N, V = 1024, 1024, 512, 128, 256
FLOPS = 3 * 2 * K * N * S

F32 = mybir.dt.float32
BF16 = mybir.dt.bfloat16
I32 = mybir.dt.int32
U32 = mybir.dt.uint32
U16 = mybir.dt.uint16
U8 = mybir.dt.uint8
FP8X4 = mybir.dt.float8_e4m3fn_x4
ALU = mybir.AluOpType
ACT = mybir.ActivationFunctionType

P = 128
PACK = 4
PASSES = K // (P * PACK)
LANES = 16
HALF_S = S // 2
HALF_V = V // 2


def tile_picked_ydehz_depth_p_kernel(
    tc, x_words, x_scales, w1, w2, w3, air, tmin, beta, offs, pos1, pos2, cen, out
):
    nc = tc.nc
    with ExitStack() as ctx:
        sb = ctx.enter_context(tc.tile_pool(name="sb", bufs=1))
        ps = ctx.enter_context(tc.psum_pool(name="ps", bufs=1))

        def sbuf(name, shape, dtype):
            return sb.tile(shape, dtype, name=name, tag=name, align_bytes=64)

        def load_list(name, src):
            t = sbuf(name, list(src.shape), U16)
            nc.sync.dma_start(t[:], src)
            return t

        def load_words(o):
            t = sbuf("x_words%d" % o, [P, T], I32)
            nc.sync.dma_start(t[:], x_words[o].rearrange("p n t -> p (n t)").bitcast(I32))
            return t

        def load_weight(name, w, o):
            t = sbuf("%s_raw%d" % (name, o), [P, PACK, N], F32)
            rows = w[o * P * PACK : (o + 1) * P * PACK, :]
            nc.sync.dma_start(t[:], rows.rearrange("(p j) m -> p j m", j=PACK))
            return t

        def round_weight(name, raw, on_scalar):
            t = sbuf(name + "_bf16", [P, N, PACK], BF16)
            dst = t[:].rearrange("p (c i) j -> p c j i", i=4)
            src = raw[:].rearrange("p j (c i) -> p c j i", i=4)
            if on_scalar:
                nc.scalar.activation(dst, src, ACT.Copy)
            else:
                nc.vector.tensor_copy(dst, src)
            return t

        def quantise(name, rounded, tag=None):
            codes = sb.tile([P, N], U32, name=name + "_codes", tag=tag or name + "_codes", align_bytes=64)
            scales = sbuf(name + "_scales", [P, N], U8)
            nc.vector.quantize_mx(
                out=codes[:].bitcast(FP8X4), scales=scales[:], in_=rounded[:].rearrange("p m j -> p (m j)")
            )
            return codes, scales

        scale_table = sbuf("scale_table", [P, T], U8)
        nc.vector.memset(scale_table[:].bitcast(I32), 0)
        offs_t = load_list("offs_t", offs)
        raw_b0 = load_weight("w3", w3, 0)
        for q in range(4):
            nc.sync.dma_start(
                scale_table[32 * q : 32 * q + 4 * PASSES, :].bitcast(I32),
                x_scales[:, 4 * q : 4 * q + 4, :].bitcast(I32),
            )
        words0 = load_words(0)
        air_t = sbuf("air_t", [P, 1], F32)
        nc.sync.dma_start(air_t[:], air)
        raw_g0 = load_weight("w2", w2, 0)
        raw_b1 = load_weight("w3", w3, 1)
        words1 = load_words(1)
        raw_g1 = load_weight("w2", w2, 1)
        raw_r0 = load_weight("w1", w1, 0)
        raw_r1 = load_weight("w1", w1, 1)
        cen_t = load_list("cen_t", cen)
        pos1_t = load_list("pos1_t", pos1)
        pos2_t = load_list("pos2_t", pos2)
        tmin_t = sbuf("tmin_t", [P, V], F32)
        nc.sync.dma_start(tmin_t[:], tmin)
        beta_t = sbuf("beta_t", [P, V], F32)
        nc.sync.dma_start(beta_t[:], beta)

        shift = sbuf("shift", [P, 1], F32)
        nc.gpsimd.tensor_scalar(shift[:], air_t[:], 10.0, 1.0, ALU.mult, ALU.add)
        root = sbuf("root", [P, 1], F32)
        nc.gpsimd.tensor_scalar(root[:], air_t[:], 38.0 / 3.0, 0.0, ALU.mult, ALU.add)

        def gather_words(o, words):
            t = sbuf("picked_words%d" % o, [P, S], U32)
            nc.vector.tensor_copy(t[:], words[:].bitcast(U32).indirect(offs_t[:]))
            return t

        picked_scales = sbuf("picked_scales", [P, S], U8)
        nc.vector.tensor_copy(picked_scales[:], scale_table[:].indirect(offs_t[:]))

        def product(bank, q, picked, o, cols):
            codes, scales = q
            nc.tensor.matmul_mx(
                out=bank[:],
                lhsT=codes[:].bitcast(FP8X4),
                lhsT_scale=scales[:],
                rhs=picked[:, cols].bitcast(FP8X4),
                rhs_scale=picked_scales[4 * o : P, cols],
                start=(o == 0),
                stop=(o == PASSES - 1),
            )

        every = slice(0, S)
        bank_b = [ps.tile([P, HALF_S], F32, name="bank_b%d" % h) for h in range(2)]
        bank_g = ps.tile([P, S], F32, name="bank_g")
        halves = [slice(0, HALF_S), slice(HALF_S, S)]
        pieces = [slice(0, 256), slice(256, 512)]
        bank_r = [ps.tile([P, c.stop - c.start], F32, name="bank_r%d" % c.start) for c in pieces]

        q = quantise("w3_0", round_weight("w3_0", raw_b0, True))
        picked0 = gather_words(0, words0)
        for bank, c in zip(bank_b, halves):
            product(bank, q, picked0, 0, c)
        q = quantise("w2_0", round_weight("w2_0", raw_g0, True))
        product(bank_g, q, picked0, 0, every)
        q = quantise("w3_1", round_weight("w3_1", raw_b1, True))
        picked1 = sbuf("picked_words1", [P, S], U32)
        for bank, c in zip(bank_b, halves):
            entries = offs_t[:, c.start // LANES : c.stop // LANES]
            nc.vector.tensor_copy(picked1[:, c], words1[:].bitcast(U32).indirect(entries))
            product(bank, q, picked1, 1, c)
        q = quantise("w2_1", round_weight("w2_1", raw_g1, True))
        product(bank_g, q, picked1, 1, every)
        rounded_r0 = round_weight("w1_0", raw_r0, True)
        rounded_r1 = round_weight("w1_1", raw_r1, False)
        q0 = quantise("w1_0", rounded_r0)
        q1 = quantise("w1_1", rounded_r1, "last")
        for bank, c in zip(bank_r, pieces):
            product(bank, q0, picked0, 0, c)
        for bank, c in zip(bank_r, pieces):
            product(bank, q1, picked1, 1, c)
        blu = sb.tile([P, S], F32, name="blu", tag="w1_raw0", align_bytes=64)
        for bank, c in zip(bank_b, halves):
            nc.scalar.activation(blu[:, c], bank[:], ACT.Tanh, bias=0.75, scale=0.5)
        grn = sbuf("grn", [P, S], F32)
        for c in halves:
            nc.scalar.activation(grn[:, c], bank_g[:, c], ACT.Tanh, bias=0.75, scale=0.5)
        red = sbuf("red", [P, S], F32)
        for bank, c in zip(bank_r, pieces):
            nc.scalar.activation(red[:, c], bank[:], ACT.Tanh, bias=0.75, scale=0.5)
        blu_cen = sb.tile([P, V], F32, name="blu_cen", tag="last", align_bytes=64)
        nc.scalar.activation(blu_cen[:], blu[:].indirect(cen_t[:]), ACT.Copy)
        blu_shifted = sb.tile([P, S], F32, name="blu_shifted", tag="w1_1_bf16", align_bytes=64)
        for c in halves:
            nc.vector.tensor_scalar(blu_shifted[:, c], blu[:, c], shift[:], None, ALU.add)
        low = sbuf("low", [P, S], F32)
        for c in halves:
            nc.vector.scalar_tensor_tensor(low[:, c], grn[:, c], shift[:], blu_shifted[:, c], ALU.add, ALU.min)
        dark = sbuf("dark", [P, S], F32)
        for c in pieces:
            nc.vector.scalar_tensor_tensor(dark[:, c], red[:, c], shift[:], low[:, c], ALU.add, ALU.min)

        NP = 4
        W = V // NP

        def part(name):
            return [sbuf("%s%d" % (name, h), [P, W], F32) for h in range(NP)]

        def fetch(name, lst, h, on_scalar):
            dst = sbuf("%s%d" % (name, h), [P, HALF_V], F32)
            w = HALF_V // LANES
            src = dark[:].indirect(lst[:, h * w : (h + 1) * w])
            if on_scalar:
                nc.scalar.activation(dst[:], src, ACT.Copy)
            else:
                nc.vector.tensor_copy(dst[:], src)
            return dst

        x, d, pn, lg, lb = [part(n) for n in ("x", "d", "pn", "lg", "lb")]
        res = [sbuf("res%d" % h, [P, HALF_V], F32) for h in range(2)]
        r = [sb.tile([P, V], F32, name="r0", tag="floor_then_colour")] + part("r")[1:]
        pair = [sbuf("pair%d" % h, [P, 2, W], F32) for h in range(NP)]
        logs = [sbuf("logs%d" % h, [P, 2, W], F32) for h in range(NP)]
        cols = [slice(h * W, (h + 1) * W) for h in range(NP)]
        g0, g1, g2 = [], [], []
        g0.append(fetch("g0", cen_t, 0, True))
        g2.append(fetch("g2", pos2_t, 0, False))
        g1.append(fetch("g1", pos1_t, 0, True))
        g2.append(fetch("g2", pos2_t, 1, False))
        g0.append(fetch("g0", cen_t, 1, True))
        g1.append(fetch("g1", pos1_t, 1, False))

        def piece(g, h):
            per = NP // 2
            return g[h // per][:, (h % per) * W : (h % per + 1) * W]

        for h in range(NP):
            nc.vector.tensor_tensor(x[h][:], piece(g2, h), piece(g0 if h < NP // 2 else g1, h), ALU.min)
        for h in range(NP):
            nc.vector.tensor_tensor(d[h][:], x[h][:], piece(g1 if h < NP // 2 else g0, h), ALU.min)
        for h in range(NP):
            nc.vector.tensor_tensor(pair[h][:, 0, :], d[h][:], d[h][:], ALU.mult)
        for h in range(NP):
            nc.vector.scalar_tensor_tensor(pn[h][:], d[h][:], root[:], d[h][:], ALU.subtract, ALU.mult)
        for h in range(NP):
            nc.vector.tensor_tensor(r[h][:, 0:W], pair[h][:, 0, :], tmin_t[:, cols[h]], ALU.mult)
        for h in range(NP):
            nc.vector.scalar_tensor_tensor(pair[h][:, 1, :], pn[h][:], -3.75, r[h][:, 0:W], ALU.mult, ALU.max)
            nc.scalar.activation(logs[h][:], pair[h][:], ACT.Ln)
        colour = sb.tile([P, V], F32, name="colour", tag="floor_then_colour")
        nc.vector.tensor_tensor(colour[:], grn[:].indirect(cen_t[:]), blu_cen[:], ALU.subtract)
        for h in range(NP):
            nc.vector.tensor_tensor(lg[h][:], logs[h][:, 1, :], logs[h][:, 0, :], ALU.subtract)
        for h in range(NP):
            nc.vector.tensor_tensor(lb[h][:], lg[h][:], beta_t[:, cols[h]], ALU.mult)
        for h in range(NP):
            nc.vector.scalar_tensor_tensor(piece(res, h), colour[:, cols[h]], 0.2, lb[h][:], ALU.mult, ALU.add)
            if (h + 1) % (NP // 2) == 0:
                u = h // (NP // 2)
                nc.sync.dma_start(out[:, u * HALF_V : (u + 1) * HALF_V], res[u][:])
